import numpy as np
import ml_dtypes


def mxq(x, axis, fmt="e4m3"):
    dtype, down = {"e4m3": (ml_dtypes.float8_e4m3fn, 7), "e5m2": (ml_dtypes.float8_e5m2, 14)}[fmt]
    v = np.moveaxis(np.asarray(x, np.float32).astype(ml_dtypes.bfloat16).astype(np.float64), axis, -1)
    blocks = v.reshape(v.shape[:-1] + (-1, 32))
    amax = np.abs(blocks).max(-1, keepdims=True)
    byte = np.maximum(np.where(amax > 0, np.frexp(amax)[1] - 1 + 127, 0) - down, 1)
    scale = np.exp2(byte - 127.0)
    codes = (blocks / scale).astype(np.float32).astype(dtype).astype(np.float64)
    return np.moveaxis((codes * scale).reshape(v.shape), -1, axis)


WIDE = False


def mx_kscale(k):
    if not WIDE:
        return np.ones(k)
    levels = np.array([30, -30])
    if k % 512:
        return np.exp2(np.random.permutation(np.resize(levels, k // 32))).repeat(32)
    a = np.empty((k // 512, 16))
    for p in range(k // 512):
        a[p, :8] = np.random.permutation(np.resize(levels, 8))
        for g in range(8):
            far = levels[np.abs(levels - a[p, g]) >= 10]
            a[p, g + 8] = far[np.random.randint(len(far))]
    return np.exp2(a.ravel()).repeat(32)


def f64(x):
    return np.asarray(x).astype(np.float64)


def striped(idx):
    return np.tile(np.asarray(idx).reshape(-1, 16).T, (8, 1)).astype(np.uint16)


def unstriped(offs):
    return offs[:16].T.reshape(-1).astype(np.int64)


E2M1 = np.array([0.0, 0.5, 1.0, 1.5, 2.0, 3.0, 4.0, 6.0, -0.0, -0.5, -1.0, -1.5, -2.0, -3.0, -4.0, -6.0])


def pack_weight(w, fmt):
    k, n = w.shape
    w = f64(np.asarray(w, np.float32).astype(ml_dtypes.bfloat16)).reshape(k // 32, 32, n)
    amax = np.abs(w).max(1)
    if fmt in ("e4m3", "e5m2"):
        byte = np.frexp(amax)[1] - 1 + 127 - (7 if fmt == "e4m3" else 14)
    else:
        mant, ex = np.frexp(amax / 6.0)
        byte = np.where(mant > 0.5, ex, ex - 1) + 127
    byte = np.clip(np.where(amax > 0, byte, 1), 1, 254)
    scaled = (w * np.exp2(127.0 - byte)[:, None, :]).reshape(k, n).astype(np.float32)
    by_word = np.ascontiguousarray(scaled.reshape(k // 512, 128, 4, n).transpose(0, 1, 3, 2))
    if fmt in ("e4m3", "e5m2"):
        words = by_word.astype(ml_dtypes.float8_e4m3fn if fmt == "e4m3" else ml_dtypes.float8_e5m2).view(np.uint8)
    else:
        c = by_word.astype(ml_dtypes.float4_e2m1fn).view(np.uint8) & 0xF
        words = (c[..., 0::2] | (c[..., 1::2] << 4)).reshape(k // 512, 128, 2 * n)
    return np.ascontiguousarray(words), np.ascontiguousarray(byte.astype(np.uint8).reshape(k // 512, 16, n))


def unpack_weight(words, scales, fmt):
    g, _, n = scales.shape
    words = np.ascontiguousarray(words).reshape(g, 128, n, -1)
    if fmt in ("e4m3", "e5m2"):
        vals = words.view(ml_dtypes.float8_e4m3fn if fmt == "e4m3" else ml_dtypes.float8_e5m2).astype(np.float64)
    else:
        nib = np.empty((g, 128, n, 4), np.uint8)
        nib[..., 0::2] = words & 0xF
        nib[..., 1::2] = words >> 4
        vals = E2M1[nib]
    vals = vals * np.repeat(np.exp2(scales.astype(np.float64) - 127.0), 8, axis=1)[..., None]
    return vals.transpose(0, 1, 3, 2).reshape(g * 512, n)


def e4m3fn_bytes(y):
    return np.clip(np.asarray(y, np.float64), -448.0, 448.0).astype(np.float32).astype(ml_dtypes.float8_e4m3fn).view(np.uint8)


def e4m3fn_values(b):
    return np.asarray(b, np.uint8).view(ml_dtypes.float8_e4m3fn).astype(np.float64)


K, V, J, N, E = 512, 2048, 512, 256, 1024


def setup_inputs():
    n = np.random.standard_normal
    idx = np.random.permutation(V)[:J]
    idx2 = np.random.permutation(E)[:J]
    fk = mx_kscale(K)
    wp = pack_weight(n((K, N)) * 1 / np.sqrt(K) / fk[:, None], "e5m2")
    w2p = pack_weight(n((K, N)) * 1 / np.sqrt(K) / fk[:, None], "e4m3")
    return {
        "ca": e4m3fn_bytes(6.0 * n((K, V))),
        "sa": (np.random.uniform(0.05, 0.15, (K, 1)) * fk[:, None]).astype(np.float32),
        "sb": (np.random.uniform(0.01, 0.03, (K, 1)) * fk[:, None]).astype(np.float32),
        "w_words": wp[0],
        "w_scales": wp[1],
        "w2_words": w2p[0],
        "w2_scales": w2p[1],
        "so": (np.random.uniform(0.5, 1.6, (N, 1))).astype(np.float32),
        "offs": striped(idx),
        "offs2": striped(idx2),
    }


def reference(ca, sa, sb, w_words, w_scales, w2_words, w2_scales, so, offs, offs2):
    idx = unstriped(offs)
    idx2 = unstriped(offs2)
    wu = unpack_weight(w_words, w_scales, "e5m2")
    w2u = unpack_weight(w2_words, w2_scales, "e4m3")
    z1 = e4m3fn_values(ca)[:, idx] * f64(sa)
    z2 = np.square(e4m3fn_values(ca)[:, idx]) * f64(sb)
    z1q = mxq(z1, 0, "e4m3")
    z2q = mxq(z2, 0, "e4m3")
    p = wu.T @ z1q + w2u.T @ z2q
    y = np.zeros((N, E))
    y[:, idx2] = p * f64(so)
    return y

@@ -1,0 +1,130 @@
+from contextlib import ExitStack
+
+import concourse.mybir as mybir
+
+K, V, J, N, E = 512, 2048, 512, 256, 1024
+FLOPS = 2 * 2 * K * N * J
+
+F32 = mybir.dt.float32
+BF16 = mybir.dt.bfloat16
+I32 = mybir.dt.int32
+U32 = mybir.dt.uint32
+U16 = mybir.dt.uint16
+U8 = mybir.dt.uint8
+FP8 = mybir.dt.float8_e4m3fn
+E4X4 = mybir.dt.float8_e4m3fn_x4
+E5X4 = mybir.dt.float8_e5m2_x4
+MULT = mybir.AluOpType.mult
+COPY = mybir.ActivationFunctionType.Copy
+
+P = 128
+PACK = 4
+HALF = 256
+CHUNK = 128
+RUN = 2
+
+
+def tile_list_moments_kernel(tc, ca, sa, sb, w_words, w_scales, w2_words, w2_scales, so, offs, offs2, out):
+    nc = tc.nc
+    with ExitStack() as ctx:
+        keep = ctx.enter_context(tc.tile_pool(name="keep", bufs=1))
+        psum = ctx.enter_context(tc.psum_pool(name="psum", bufs=1))
+
+        pick = keep.tile([P, J // 16], U16, name="pick")
+        put = keep.tile([P, J // 16], U16, name="put")
+        nc.sync.dma_start(pick[:], offs)
+        ca_planes = ca.rearrange("(p t) v -> t p v", t=PACK)
+        table = [keep.tile([P, V], U8, name="table%d" % t) for t in range(PACK)]
+        for t in range(PACK):
+            nc.sync.dma_start(table[t][:], ca_planes[t])
+
+        staged = []
+        for name, sc in (("w", w_scales), ("w2", w2_scales)):
+            st = keep.tile([4, 4, N // 4], I32, name=name + "_staged")
+            nc.scalar.dma_start(st[:], sc[0].bitcast(I32).rearrange("(q r) c -> r q c", r=4))
+            staged.append(st)
+        step = keep.tile([P, PACK], F32, name="step")
+        step2 = keep.tile([P, PACK], F32, name="step2")
+        nc.scalar.dma_start(step2[:], sb.rearrange("(p t) o -> p (t o)", t=PACK))
+        nc.scalar.dma_start(step[:], sa.rearrange("(p t) o -> p (t o)", t=PACK))
+
+        words = []
+        planes = []
+        for name, wd in (("w", w_words), ("w2", w2_words)):
+            wt = keep.tile([P, N], I32, name=name + "_words", align_bytes=64)
+            nc.sync.dma_start(wt[:], wd[0].rearrange("p n t -> p (n t)").bitcast(I32))
+            words.append(wt)
+            pl = keep.tile([P, N], U8, name=name + "_plane", align_bytes=64)
+            nc.vector.memset(pl[:].bitcast(I32), 0)
+            planes.append(pl)
+        nc.sync.dma_start(put[:], offs2)
+        weight = keep.tile([P, 2], F32, name="weight")
+        with nc.allow_non_contiguous_dma(reason="one float32 a row"):
+            nc.sync.dma_start(weight[:], so.rearrange("(h p) o -> p (h o)", p=P))
+
+        pages = [keep.tile([P, E], F32, name="page%d" % h) for h in range(2)]
+        for h in range(2):
+            nc.vector.memset(pages[h][:], 0.0)
+        for x in range(2):
+            for q in range(4):
+                nc.vector.tensor_copy(planes[x][32 * q : 32 * q + 4, :].bitcast(I32), staged[x][:, q, :])
+
+        plain = [keep.tile([P, PACK, HALF], F32, name="plain%d" % g) for g in range(2)]
+        scaled = [keep.tile([P, PACK, HALF], F32, name="scaled%d" % g) for g in range(2)]
+
+        def look_up(g, t, tag):
+            picked = keep.tile([P, HALF], U8, name="picked%d%d" % (g, t), tag=tag, align_bytes=64)
+            cols = slice(g * HALF // 16, (g + 1) * HALF // 16)
+            nc.vector.tensor_copy(picked[:], table[t][:].indirect(pick[:, cols]))
+            nc.scalar.copy(plain[g][:, t, :], picked[:].bitcast(FP8))
+            nc.scalar.activation(scaled[g][:, t, :], picked[:].bitcast(FP8), COPY, scale=step2[:, t : t + 1])
+
+        def chunk(c, tags, copier):
+            g, j0 = divmod(c * CHUNK, HALF)
+            z = [keep.tile([P, CHUNK, PACK], BF16, name="z%d%d" % (c, x), tag=tags[x], align_bytes=64) for x in range(2)]
+            codes = [keep.tile([P, CHUNK], U32, name="codes%d%d" % (c, x), align_bytes=64) for x in range(2)]
+            scales = [keep.tile([P, CHUNK], U8, name="scales%d%d" % (c, x), align_bytes=64) for x in range(2)]
+            walk_in = "p t (c i) -> p c t i"
+            walk_out = "p (c i) t -> p c t i"
+            c_view = plain[g][:, :, j0 : j0 + CHUNK].rearrange(walk_in, i=RUN)
+            u_view = scaled[g][:, :, j0 : j0 + CHUNK].rearrange(walk_in, i=RUN)
+            s_view = step[:].unsqueeze(1).unsqueeze(3).to_broadcast([P, CHUNK // RUN, PACK, RUN])
+            nc.vector.tensor_tensor(z[0][:].rearrange(walk_out, i=RUN), c_view, s_view, MULT)
+            nc.vector.tensor_tensor(z[1][:].rearrange(walk_out, i=RUN), c_view, u_view, MULT)
+            for x in range(2):
+                nc.vector.quantize_mx(out=codes[x][:].bitcast(E4X4), scales=scales[x][:], in_=z[x][:].rearrange("p j t -> p (j t)"))
+            acc = [psum.tile([P, CHUNK], F32, name="acc%d%d" % (c, h)) for h in range(2)]
+            for x, fmt in ((0, E5X4), (1, E4X4)):
+                for h in range(2):
+                    rows = slice(h * P, (h + 1) * P)
+                    nc.tensor.matmul_mx(
+                        out=acc[h][:],
+                        lhsT=words[x][:, rows].bitcast(fmt),
+                        lhsT_scale=planes[x][:, rows],
+                        rhs=codes[x][:].bitcast(E4X4),
+                        rhs_scale=scales[x][:],
+                        start=(x == 0),
+                        stop=(x == 1),
+                    )
+            return acc
+
+        def place(c, acc, copier):
+            cols = slice(c * CHUNK // 16, (c + 1) * CHUNK // 16)
+            for h in range(2):
+                sums = keep.tile([P, CHUNK], F32, name="sums%d%d" % (c, h))
+                copier(sums[:], acc[h][:])
+                nc.scalar.activation(pages[h][:].indirect(put[:, cols]), sums[:], COPY, scale=weight[:, h : h + 1])
+
+        for t in range(PACK):
+            look_up(0, t, "a%d" % t)
+        look_up(1, 0, "a2")
+        acc0 = chunk(0, ("z00", "z01"), None)
+        look_up(1, 1, "z01")
+        look_up(1, 2, "z00")
+        place(0, acc0, nc.vector.tensor_copy)
+        look_up(1, 3, "a3")
+        for c in range(1, 4):
+            acc = chunk(c, ("z01" if c == 1 else "z%d0" % c, "z%d1" % c), None)
+            place(c, acc, nc.vector.tensor_copy)
+        for h in range(2):
+            nc.sync.dma_start(out[h * P : (h + 1) * P, :], pages[h][:])

@@ -21,7 +21,7 @@ P = 128
 PACK = 4
 HALF = 256
 CHUNK = 128
-RUN = 2
+RUN = 4
 
 
 def tile_list_moments_kernel(tc, ca, sa, sb, w_words, w_scales, w2_words, w2_scales, so, offs, offs2, out):
@@ -32,21 +32,19 @@ def tile_list_moments_kernel(tc, ca, sa, sb, w_words, w_scales, w2_words, w2_sca
 
         pick = keep.tile([P, J // 16], U16, name="pick")
         put = keep.tile([P, J // 16], U16, name="put")
-        nc.sync.dma_start(pick[:], offs)
         ca_planes = ca.rearrange("(p t) v -> t p v", t=PACK)
         table = [keep.tile([P, V], U8, name="table%d" % t) for t in range(PACK)]
         for t in range(PACK):
             nc.sync.dma_start(table[t][:], ca_planes[t])
+            if t == 0:
+                nc.sync.dma_start(pick[:], offs)
 
-        staged = []
-        for name, sc in (("w", w_scales), ("w2", w2_scales)):
-            st = keep.tile([4, 4, N // 4], I32, name=name + "_staged")
-            nc.scalar.dma_start(st[:], sc[0].bitcast(I32).rearrange("(q r) c -> r q c", r=4))
-            staged.append(st)
-        step = keep.tile([P, PACK], F32, name="step")
-        step2 = keep.tile([P, PACK], F32, name="step2")
-        nc.scalar.dma_start(step2[:], sb.rearrange("(p t) o -> p (t o)", t=PACK))
-        nc.scalar.dma_start(step[:], sa.rearrange("(p t) o -> p (t o)", t=PACK))
+        loaded = keep.tile([P, 2, 2 * PACK], F32, name="loaded")
+        for x, src in enumerate((sa, sb)):
+            nc.scalar.dma_start(loaded[:, x, :PACK], src.rearrange("(p t) o -> p (t o)", t=PACK))
+        steps = keep.tile([P, 2, PACK], F32, name="steps")
+        nc.vector.tensor_copy(steps[:], loaded[:, :, :PACK])
+        step, step2 = steps[:, 0, :], steps[:, 1, :]
 
         words = []
         planes = []
@@ -57,6 +55,9 @@ def tile_list_moments_kernel(tc, ca, sa, sb, w_words, w_scales, w2_words, w2_sca
             pl = keep.tile([P, N], U8, name=name + "_plane", align_bytes=64)
             nc.vector.memset(pl[:].bitcast(I32), 0)
             planes.append(pl)
+        for x, sc in enumerate((w_scales, w2_scales)):
+            for q in range(4):
+                nc.sync.dma_start(planes[x][32 * q : 32 * q + 4, :].bitcast(I32), sc[0, 4 * q : 4 * q + 4, :].bitcast(I32))
         nc.sync.dma_start(put[:], offs2)
         weight = keep.tile([P, 2], F32, name="weight")
         with nc.allow_non_contiguous_dma(reason="one float32 a row"):
@@ -65,34 +66,38 @@ def tile_list_moments_kernel(tc, ca, sa, sb, w_words, w_scales, w2_words, w2_sca
         pages = [keep.tile([P, E], F32, name="page%d" % h) for h in range(2)]
         for h in range(2):
             nc.vector.memset(pages[h][:], 0.0)
-        for x in range(2):
-            for q in range(4):
-                nc.vector.tensor_copy(planes[x][32 * q : 32 * q + 4, :].bitcast(I32), staged[x][:, q, :])
 
-        plain = [keep.tile([P, PACK, HALF], F32, name="plain%d" % g) for g in range(2)]
+        last = PACK - 1
+        picked = [keep.tile([P, last, HALF], U8, name="picked%d" % g) for g in range(2)]
         scaled = [keep.tile([P, PACK, HALF], F32, name="scaled%d" % g) for g in range(2)]
+        z1 = [keep.tile([P, PACK, HALF], BF16, name="z1_%d" % g) for g in range(2)]
 
-        def look_up(g, t, tag):
-            picked = keep.tile([P, HALF], U8, name="picked%d%d" % (g, t), tag=tag, align_bytes=64)
+        def look_up(g, t, dst, on_scalar):
             cols = slice(g * HALF // 16, (g + 1) * HALF // 16)
-            nc.vector.tensor_copy(picked[:], table[t][:].indirect(pick[:, cols]))
-            nc.scalar.copy(plain[g][:, t, :], picked[:].bitcast(FP8))
-            nc.scalar.activation(scaled[g][:, t, :], picked[:].bitcast(FP8), COPY, scale=step2[:, t : t + 1])
+            nc.vector.tensor_copy(dst, table[t][:].indirect(pick[:, cols]))
+            for prod, fac in ((scaled[g], step2), (z1[g], step)):
+                if on_scalar:
+                    nc.scalar.activation(prod[:, t, :], dst.bitcast(FP8), COPY, scale=fac[:, t : t + 1])
+                else:
+                    nc.vector.tensor_scalar(prod[:, t, :], dst.bitcast(FP8), fac[:, t : t + 1], None, MULT)
 
-        def chunk(c, tags, copier):
-            g, j0 = divmod(c * CHUNK, HALF)
-            z = [keep.tile([P, CHUNK, PACK], BF16, name="z%d%d" % (c, x), tag=tags[x], align_bytes=64) for x in range(2)]
+        def flat(ap):
+            return ap.rearrange("p t j -> p (t j)")
+
+        def weave(c, x, src, copier, tag):
+            j0 = (c * CHUNK) % HALF
+            z = keep.tile([P, CHUNK, PACK], BF16, name="woven%d%d" % (c, x), tag=tag, align_bytes=64)
+            copier(
+                z[:].rearrange("p (c i) t -> p c t i", i=RUN),
+                src[:, :, j0 : j0 + CHUNK].rearrange("p t (c i) -> p c t i", i=RUN),
+            )
+            return z
+
+        def multiply(c, woven):
             codes = [keep.tile([P, CHUNK], U32, name="codes%d%d" % (c, x), align_bytes=64) for x in range(2)]
             scales = [keep.tile([P, CHUNK], U8, name="scales%d%d" % (c, x), align_bytes=64) for x in range(2)]
-            walk_in = "p t (c i) -> p c t i"
-            walk_out = "p (c i) t -> p c t i"
-            c_view = plain[g][:, :, j0 : j0 + CHUNK].rearrange(walk_in, i=RUN)
-            u_view = scaled[g][:, :, j0 : j0 + CHUNK].rearrange(walk_in, i=RUN)
-            s_view = step[:].unsqueeze(1).unsqueeze(3).to_broadcast([P, CHUNK // RUN, PACK, RUN])
-            nc.vector.tensor_tensor(z[0][:].rearrange(walk_out, i=RUN), c_view, s_view, MULT)
-            nc.vector.tensor_tensor(z[1][:].rearrange(walk_out, i=RUN), c_view, u_view, MULT)
             for x in range(2):
-                nc.vector.quantize_mx(out=codes[x][:].bitcast(E4X4), scales=scales[x][:], in_=z[x][:].rearrange("p j t -> p (j t)"))
+                nc.vector.quantize_mx(out=codes[x][:].bitcast(E4X4), scales=scales[x][:], in_=woven[x][:].rearrange("p j t -> p (j t)"))
             acc = [psum.tile([P, CHUNK], F32, name="acc%d%d" % (c, h)) for h in range(2)]
             for x, fmt in ((0, E5X4), (1, E4X4)):
                 for h in range(2):
@@ -108,23 +113,36 @@ def tile_list_moments_kernel(tc, ca, sa, sb, w_words, w_scales, w2_words, w2_sca
                     )
             return acc
 
-        def place(c, acc, copier):
+        def place(c, acc, copier, tag):
             cols = slice(c * CHUNK // 16, (c + 1) * CHUNK // 16)
+            sums = [keep.tile([P, CHUNK], F32, name="sums%d%d" % (c, h), tag="%s%d" % (tag, h)) for h in range(2)]
             for h in range(2):
-                sums = keep.tile([P, CHUNK], F32, name="sums%d%d" % (c, h))
-                copier(sums[:], acc[h][:])
-                nc.scalar.activation(pages[h][:].indirect(put[:, cols]), sums[:], COPY, scale=weight[:, h : h + 1])
+                copier(sums[h][:], acc[h][:])
+            for h in range(2):
+                nc.scalar.activation(pages[h][:].indirect(put[:, cols]), sums[h][:], COPY, scale=weight[:, h : h + 1])
 
-        for t in range(PACK):
-            look_up(0, t, "a%d" % t)
-        look_up(1, 0, "a2")
-        acc0 = chunk(0, ("z00", "z01"), None)
-        look_up(1, 1, "z01")
-        look_up(1, 2, "z00")
-        place(0, acc0, nc.vector.tensor_copy)
-        look_up(1, 3, "a3")
-        for c in range(1, 4):
-            acc = chunk(c, ("z01" if c == 1 else "z%d0" % c, "z%d1" % c), None)
-            place(c, acc, nc.vector.tensor_copy)
+        for t in range(last):
+            for g in range(2):
+                look_up(g, t, picked[g][:, t, :], True)
+        tail0 = keep.tile([P, HALF], U8, name="tail0")
+        look_up(0, last, tail0[:], True)
+        z2a = keep.tile([P, PACK, HALF], BF16, name="z2a")
+        nc.vector.tensor_tensor(flat(z2a[:, :last, :]), flat(picked[0][:]).bitcast(FP8), flat(scaled[0][:, :last, :]), MULT)
+        nc.vector.tensor_tensor(z2a[:, last, :], tail0[:].bitcast(FP8), scaled[0][:, last, :], MULT)
+
+        woven0 = [weave(0, 0, z1[0], nc.vector.tensor_copy, "first0"), weave(0, 1, z2a, nc.vector.tensor_copy, "first1")]
+        acc0 = multiply(0, woven0)
+        woven1 = [weave(1, 0, z1[0], nc.scalar.copy, "woven10"), weave(1, 1, z2a, nc.scalar.copy, "woven11")]
+        place(0, acc0, nc.scalar.copy, "early")
+        acc1 = multiply(1, woven1)
+        tail1 = keep.tile([P, HALF], U8, name="tail1", tag="first0", align_bytes=64)
+        look_up(1, last, tail1[:], False)
+        z2b = keep.tile([P, PACK, HALF], BF16, name="z2b", tag="first1", align_bytes=64)
+        nc.vector.tensor_tensor(flat(z2b[:, :last, :]), flat(picked[1][:]).bitcast(FP8), flat(scaled[1][:, :last, :]), MULT)
+        nc.vector.tensor_tensor(z2b[:, last, :], tail1[:].bitcast(FP8), scaled[1][:, last, :], MULT)
+        place(1, acc1, nc.scalar.copy, "early")
+        for c in range(2, 4):
+            woven = [weave(c, x, src, nc.vector.tensor_copy, "woven%d%d" % (c, x)) for x, src in enumerate((z1[1], z2b))]
+            place(c, multiply(c, woven), nc.vector.tensor_copy, "late%d" % c)
         for h in range(2):
             nc.sync.dma_start(out[h * P : (h + 1) * P, :], pages[h][:])

@@ -46,18 +46,21 @@ def tile_list_moments_kernel(tc, ca, sa, sb, w_words, w_scales, w2_words, w2_sca
         nc.vector.tensor_copy(steps[:], loaded[:, :, :PACK])
         step, step2 = steps[:, 0, :], steps[:, 1, :]
 
-        words = []
-        planes = []
-        for name, wd in (("w", w_words), ("w2", w2_words)):
-            wt = keep.tile([P, N], I32, name=name + "_words", align_bytes=64)
-            nc.sync.dma_start(wt[:], wd[0].rearrange("p n t -> p (n t)").bitcast(I32))
-            words.append(wt)
-            pl = keep.tile([P, N], U8, name=name + "_plane", align_bytes=64)
-            nc.vector.memset(pl[:].bitcast(I32), 0)
-            planes.append(pl)
-        for x, sc in enumerate((w_scales, w2_scales)):
+        words = [keep.tile([P, N], I32, name="words%d" % x, align_bytes=64) for x in range(2)]
+        planes = [keep.tile([P, N], U8, name="plane%d" % x, align_bytes=64) for x in range(2)]
+
+        def load_words(x, src):
+            nc.sync.dma_start(words[x][:], src[0].rearrange("p n t -> p (n t)").bitcast(I32))
+
+        def load_scales(x, src):
+            nc.vector.memset(planes[x][:].bitcast(I32), 0)
             for q in range(4):
-                nc.sync.dma_start(planes[x][32 * q : 32 * q + 4, :].bitcast(I32), sc[0, 4 * q : 4 * q + 4, :].bitcast(I32))
+                nc.sync.dma_start(planes[x][32 * q : 32 * q + 4, :].bitcast(I32), src[0, 4 * q : 4 * q + 4, :].bitcast(I32))
+
+        load_words(0, w_words)
+        load_scales(1, w2_scales)
+        load_words(1, w2_words)
+        load_scales(0, w_scales)
         nc.sync.dma_start(put[:], offs2)
         weight = keep.tile([P, 2], F32, name="weight")
         with nc.allow_non_contiguous_dma(reason="one float32 a row"):
@@ -68,18 +71,23 @@ def tile_list_moments_kernel(tc, ca, sa, sb, w_words, w_scales, w2_words, w2_sca
             nc.vector.memset(pages[h][:], 0.0)
 
         last = PACK - 1
-        picked = [keep.tile([P, last, HALF], U8, name="picked%d" % g) for g in range(2)]
+        picked = keep.tile([P, last, HALF], U8, name="picked", tag="picked")
         scaled = [keep.tile([P, PACK, HALF], F32, name="scaled%d" % g) for g in range(2)]
         z1 = [keep.tile([P, PACK, HALF], BF16, name="z1_%d" % g) for g in range(2)]
 
-        def look_up(g, t, dst, on_scalar):
+        def on_scalar(prod, codes, fac):
+            nc.scalar.activation(prod, codes.bitcast(FP8), COPY, scale=fac)
+
+        def on_vector(prod, codes, fac):
+            nc.vector.tensor_scalar(prod, codes.bitcast(FP8), fac, None, MULT)
+
+        def gather(g, t, dst):
             cols = slice(g * HALF // 16, (g + 1) * HALF // 16)
             nc.vector.tensor_copy(dst, table[t][:].indirect(pick[:, cols]))
-            for prod, fac in ((scaled[g], step2), (z1[g], step)):
-                if on_scalar:
-                    nc.scalar.activation(prod[:, t, :], dst.bitcast(FP8), COPY, scale=fac[:, t : t + 1])
-                else:
-                    nc.vector.tensor_scalar(prod[:, t, :], dst.bitcast(FP8), fac[:, t : t + 1], None, MULT)
+
+        def scale(g, t, src, square_by, plain_by):
+            square_by(scaled[g][:, t, :], src, step2[:, t : t + 1])
+            plain_by(z1[g][:, t, :], src, step[:, t : t + 1])
 
         def flat(ap):
             return ap.rearrange("p t j -> p (t j)")
@@ -113,36 +121,51 @@ def tile_list_moments_kernel(tc, ca, sa, sb, w_words, w_scales, w2_words, w2_sca
                     )
             return acc
 
-        def place(c, acc, copier, tag):
-            cols = slice(c * CHUNK // 16, (c + 1) * CHUNK // 16)
+        def empty(c, acc, copier, tag):
             sums = [keep.tile([P, CHUNK], F32, name="sums%d%d" % (c, h), tag="%s%d" % (tag, h)) for h in range(2)]
             for h in range(2):
                 copier(sums[h][:], acc[h][:])
+            return sums
+
+        def place(c, sums):
+            cols = slice(c * CHUNK // 16, (c + 1) * CHUNK // 16)
             for h in range(2):
                 nc.scalar.activation(pages[h][:].indirect(put[:, cols]), sums[h][:], COPY, scale=weight[:, h : h + 1])
 
         for t in range(last):
-            for g in range(2):
-                look_up(g, t, picked[g][:, t, :], True)
-        tail0 = keep.tile([P, HALF], U8, name="tail0")
-        look_up(0, last, tail0[:], True)
-        z2a = keep.tile([P, PACK, HALF], BF16, name="z2a")
-        nc.vector.tensor_tensor(flat(z2a[:, :last, :]), flat(picked[0][:]).bitcast(FP8), flat(scaled[0][:, :last, :]), MULT)
-        nc.vector.tensor_tensor(z2a[:, last, :], tail0[:].bitcast(FP8), scaled[0][:, last, :], MULT)
+            gather(0, t, picked[:, t, :])
+            scale(0, t, picked[:, t, :], on_scalar, on_scalar)
+        tail = keep.tile([P, HALF], U8, name="tail")
+        gather(0, last, tail[:])
+        scale(0, last, tail[:], on_scalar, on_scalar)
+        later = {3: keep.tile([P, HALF], U8, name="later3")}
+        gather(1, 3, later[3][:])
+        z2a = keep.tile([P, PACK, HALF], BF16, name="z2a", tag="z2")
+        nc.vector.tensor_tensor(flat(z2a[:, :last, :]), flat(picked[:]).bitcast(FP8), flat(scaled[0][:, :last, :]), MULT)
+        nc.vector.tensor_tensor(z2a[:, last, :], tail[:].bitcast(FP8), scaled[0][:, last, :], MULT)
+        later[2] = keep.tile([P, HALF], U8, name="later2", tag="picked")
+        gather(1, 2, later[2][:])
 
-        woven0 = [weave(0, 0, z1[0], nc.vector.tensor_copy, "first0"), weave(0, 1, z2a, nc.vector.tensor_copy, "first1")]
+        woven0 = [weave(0, 0, z1[0], nc.scalar.copy, "first0"), weave(0, 1, z2a, nc.vector.tensor_copy, "first1")]
         acc0 = multiply(0, woven0)
-        woven1 = [weave(1, 0, z1[0], nc.scalar.copy, "woven10"), weave(1, 1, z2a, nc.scalar.copy, "woven11")]
-        place(0, acc0, nc.scalar.copy, "early")
-        acc1 = multiply(1, woven1)
-        tail1 = keep.tile([P, HALF], U8, name="tail1", tag="first0", align_bytes=64)
-        look_up(1, last, tail1[:], False)
-        z2b = keep.tile([P, PACK, HALF], BF16, name="z2b", tag="first1", align_bytes=64)
-        nc.vector.tensor_tensor(flat(z2b[:, :last, :]), flat(picked[1][:]).bitcast(FP8), flat(scaled[1][:, :last, :]), MULT)
-        nc.vector.tensor_tensor(z2b[:, last, :], tail1[:].bitcast(FP8), scaled[1][:, last, :], MULT)
-        place(1, acc1, nc.scalar.copy, "early")
+        scale(1, 3, later[3][:], on_scalar, on_scalar)
+        woven11 = weave(1, 1, z2a, nc.scalar.copy, "woven11")
+        woven10 = weave(1, 0, z1[0], nc.scalar.copy, "woven10")
+        scale(1, 2, later[2][:], on_scalar, on_scalar)
+        for t in (1, 0):
+            later[t] = keep.tile([P, HALF], U8, name="later%d" % t, tag="first%d" % (1 - t), align_bytes=64)
+            gather(1, t, later[t][:])
+        sums0 = empty(0, acc0, nc.scalar.copy, "early")
+        acc1 = multiply(1, [woven10, woven11])
+        scale(1, 1, later[1][:], on_scalar, on_vector)
+        place(0, sums0)
+        scale(1, 0, later[0][:], on_vector, on_vector)
+        z2b = keep.tile([P, PACK, HALF], BF16, name="z2b", tag="z2")
+        for t in (3, 2, 1, 0):
+            nc.vector.tensor_tensor(z2b[:, t, :], later[t][:].bitcast(FP8), scaled[1][:, t, :], MULT)
+        place(1, empty(1, acc1, nc.scalar.copy, "early"))
         for c in range(2, 4):
             woven = [weave(c, x, src, nc.vector.tensor_copy, "woven%d%d" % (c, x)) for x, src in enumerate((z1[1], z2b))]
-            place(c, multiply(c, woven), nc.vector.tensor_copy, "late%d" % c)
-        for h in range(2):
-            nc.sync.dma_start(out[h * P : (h + 1) * P, :], pages[h][:])
+            place(c, empty(c, multiply(c, woven), nc.vector.tensor_copy, "late%d" % c))
+        nc.sync.dma_start(out[:P, :], pages[0][:])
+        nc.sync.dma_start(out[P:, :], pages[1][:])

@@ -34,17 +34,17 @@ def tile_list_moments_kernel(tc, ca, sa, sb, w_words, w_scales, w2_words, w2_sca
         put = keep.tile([P, J // 16], U16, name="put")
         ca_planes = ca.rearrange("(p t) v -> t p v", t=PACK)
         table = [keep.tile([P, V], U8, name="table%d" % t) for t in range(PACK)]
-        for t in range(PACK):
-            nc.sync.dma_start(table[t][:], ca_planes[t])
-            if t == 0:
-                nc.sync.dma_start(pick[:], offs)
-
+        nc.sync.dma_start(table[0][:], ca_planes[0])
+        nc.sync.dma_start(pick[:], offs)
         loaded = keep.tile([P, 2, 2 * PACK], F32, name="loaded")
         for x, src in enumerate((sa, sb)):
-            nc.scalar.dma_start(loaded[:, x, :PACK], src.rearrange("(p t) o -> p (t o)", t=PACK))
+            nc.sync.dma_start(loaded[:, x, :PACK], src.rearrange("(p t) o -> p (t o)", t=PACK))
         steps = keep.tile([P, 2, PACK], F32, name="steps")
         nc.vector.tensor_copy(steps[:], loaded[:, :, :PACK])
         step, step2 = steps[:, 0, :], steps[:, 1, :]
+
+        for t in range(1, PACK):
+            nc.sync.dma_start(table[t][:], ca_planes[t])
 
         words = [keep.tile([P, N], I32, name="words%d" % x, align_bytes=64) for x in range(2)]
         planes = [keep.tile([P, N], U8, name="plane%d" % x, align_bytes=64) for x in range(2)]
@@ -57,9 +57,9 @@ def tile_list_moments_kernel(tc, ca, sa, sb, w_words, w_scales, w2_words, w2_sca
             for q in range(4):
                 nc.sync.dma_start(planes[x][32 * q : 32 * q + 4, :].bitcast(I32), src[0, 4 * q : 4 * q + 4, :].bitcast(I32))
 
-        load_words(0, w_words)
         load_scales(1, w2_scales)
         load_words(1, w2_words)
+        load_words(0, w_words)
         load_scales(0, w_scales)
         nc.sync.dma_start(put[:], offs2)
         weight = keep.tile([P, 2], F32, name="weight")
@@ -157,14 +157,15 @@ def tile_list_moments_kernel(tc, ca, sa, sb, w_words, w_scales, w2_words, w2_sca
             gather(1, t, later[t][:])
         sums0 = empty(0, acc0, nc.scalar.copy, "early")
         acc1 = multiply(1, [woven10, woven11])
-        scale(1, 1, later[1][:], on_scalar, on_vector)
+        scale(1, 1, later[1][:], on_vector, on_vector)
         place(0, sums0)
         scale(1, 0, later[0][:], on_vector, on_vector)
         z2b = keep.tile([P, PACK, HALF], BF16, name="z2b", tag="z2")
-        for t in (3, 2, 1, 0):
-            nc.vector.tensor_tensor(z2b[:, t, :], later[t][:].bitcast(FP8), scaled[1][:, t, :], MULT)
         place(1, empty(1, acc1, nc.scalar.copy, "early"))
         for c in range(2, 4):
+            cols = slice((c - 2) * CHUNK, (c - 1) * CHUNK)
+            for t in (3, 2, 1, 0):
+                nc.vector.tensor_tensor(z2b[:, t, cols], later[t][:, cols].bitcast(FP8), scaled[1][:, t, cols], MULT)
             woven = [weave(c, x, src, nc.vector.tensor_copy, "woven%d%d" % (c, x)) for x, src in enumerate((z1[1], z2b))]
             place(c, empty(c, multiply(c, woven), nc.vector.tensor_copy, "late%d" % c))
         nc.sync.dma_start(out[:P, :], pages[0][:])

from contextlib import ExitStack

import concourse.mybir as mybir

K, V, J, N, E = 512, 2048, 512, 256, 1024
FLOPS = 2 * 2 * K * N * J

F32 = mybir.dt.float32
BF16 = mybir.dt.bfloat16
I32 = mybir.dt.int32
U32 = mybir.dt.uint32
U16 = mybir.dt.uint16
U8 = mybir.dt.uint8
FP8 = mybir.dt.float8_e4m3fn
E4X4 = mybir.dt.float8_e4m3fn_x4
E5X4 = mybir.dt.float8_e5m2_x4
MULT = mybir.AluOpType.mult
COPY = mybir.ActivationFunctionType.Copy

P = 128
PACK = 4
HALF = 256
CHUNK = 128
RUN = 4


def tile_list_moments_kernel(tc, ca, sa, sb, w_words, w_scales, w2_words, w2_scales, so, offs, offs2, out):
    nc = tc.nc
    with ExitStack() as ctx:
        keep = ctx.enter_context(tc.tile_pool(name="keep", bufs=1))
        psum = ctx.enter_context(tc.psum_pool(name="psum", bufs=1))

        pick = keep.tile([P, J // 16], U16, name="pick")
        put = keep.tile([P, J // 16], U16, name="put")
        ca_planes = ca.rearrange("(p t) v -> t p v", t=PACK)
        table = [keep.tile([P, V], U8, name="table%d" % t) for t in range(PACK)]
        nc.sync.dma_start(table[0][:], ca_planes[0])
        nc.sync.dma_start(pick[:], offs)
        loaded = keep.tile([P, 2, 2 * PACK], F32, name="loaded")
        for x, src in enumerate((sa, sb)):
            nc.sync.dma_start(loaded[:, x, :PACK], src.rearrange("(p t) o -> p (t o)", t=PACK))
        steps = keep.tile([P, 2, PACK], F32, name="steps")
        nc.vector.tensor_copy(steps[:], loaded[:, :, :PACK])
        step, step2 = steps[:, 0, :], steps[:, 1, :]

        for t in range(1, PACK):
            nc.sync.dma_start(table[t][:], ca_planes[t])

        words = [keep.tile([P, N], I32, name="words%d" % x, align_bytes=64) for x in range(2)]
        planes = [keep.tile([P, N], U8, name="plane%d" % x, align_bytes=64) for x in range(2)]

        def load_words(x, src):
            nc.sync.dma_start(words[x][:], src[0].rearrange("p n t -> p (n t)").bitcast(I32))

        def load_scales(x, src):
            nc.vector.memset(planes[x][:].bitcast(I32), 0)
            for q in range(4):
                nc.sync.dma_start(planes[x][32 * q : 32 * q + 4, :].bitcast(I32), src[0, 4 * q : 4 * q + 4, :].bitcast(I32))

        load_scales(1, w2_scales)
        load_words(1, w2_words)
        load_words(0, w_words)
        load_scales(0, w_scales)
        nc.sync.dma_start(put[:], offs2)
        weight = keep.tile([P, 2], F32, name="weight")
        with nc.allow_non_contiguous_dma(reason="one float32 a row"):
            nc.sync.dma_start(weight[:], so.rearrange("(h p) o -> p (h o)", p=P))

        pages = [keep.tile([P, E], F32, name="page%d" % h) for h in range(2)]
        for h in range(2):
            nc.vector.memset(pages[h][:], 0.0)

        last = PACK - 1
        picked = keep.tile([P, last, HALF], U8, name="picked", tag="picked")
        scaled = [keep.tile([P, PACK, HALF], F32, name="scaled%d" % g) for g in range(2)]
        z1 = [keep.tile([P, PACK, HALF], BF16, name="z1_%d" % g) for g in range(2)]

        def on_scalar(prod, codes, fac):
            nc.scalar.activation(prod, codes.bitcast(FP8), COPY, scale=fac)

        def on_vector(prod, codes, fac):
            nc.vector.tensor_scalar(prod, codes.bitcast(FP8), fac, None, MULT)

        def gather(g, t, dst):
            cols = slice(g * HALF // 16, (g + 1) * HALF // 16)
            nc.vector.tensor_copy(dst, table[t][:].indirect(pick[:, cols]))

        def scale(g, t, src, square_by, plain_by):
            square_by(scaled[g][:, t, :], src, step2[:, t : t + 1])
            plain_by(z1[g][:, t, :], src, step[:, t : t + 1])

        def flat(ap):
            return ap.rearrange("p t j -> p (t j)")

        def weave(c, x, src, copier, tag):
            j0 = (c * CHUNK) % HALF
            z = keep.tile([P, CHUNK, PACK], BF16, name="woven%d%d" % (c, x), tag=tag, align_bytes=64)
            copier(
                z[:].rearrange("p (c i) t -> p c t i", i=RUN),
                src[:, :, j0 : j0 + CHUNK].rearrange("p t (c i) -> p c t i", i=RUN),
            )
            return z

        def multiply(c, woven):
            codes = [keep.tile([P, CHUNK], U32, name="codes%d%d" % (c, x), align_bytes=64) for x in range(2)]
            scales = [keep.tile([P, CHUNK], U8, name="scales%d%d" % (c, x), align_bytes=64) for x in range(2)]
            for x in range(2):
                nc.vector.quantize_mx(out=codes[x][:].bitcast(E4X4), scales=scales[x][:], in_=woven[x][:].rearrange("p j t -> p (j t)"))
            acc = [psum.tile([P, CHUNK], F32, name="acc%d%d" % (c, h)) for h in range(2)]
            for x, fmt in ((0, E5X4), (1, E4X4)):
                for h in range(2):
                    rows = slice(h * P, (h + 1) * P)
                    nc.tensor.matmul_mx(
                        out=acc[h][:],
                        lhsT=words[x][:, rows].bitcast(fmt),
                        lhsT_scale=planes[x][:, rows],
                        rhs=codes[x][:].bitcast(E4X4),
                        rhs_scale=scales[x][:],
                        start=(x == 0),
                        stop=(x == 1),
                    )
            return acc

        def empty(c, acc, copier, tag):
            sums = [keep.tile([P, CHUNK], F32, name="sums%d%d" % (c, h), tag="%s%d" % (tag, h)) for h in range(2)]
            for h in range(2):
                copier(sums[h][:], acc[h][:])
            return sums

        def place(c, sums):
            cols = slice(c * CHUNK // 16, (c + 1) * CHUNK // 16)
            for h in range(2):
                nc.scalar.activation(pages[h][:].indirect(put[:, cols]), sums[h][:], COPY, scale=weight[:, h : h + 1])

        for t in range(last):
            gather(0, t, picked[:, t, :])
            scale(0, t, picked[:, t, :], on_scalar, on_scalar)
        tail = keep.tile([P, HALF], U8, name="tail")
        gather(0, last, tail[:])
        scale(0, last, tail[:], on_scalar, on_scalar)
        later = {3: keep.tile([P, HALF], U8, name="later3")}
        gather(1, 3, later[3][:])
        z2a = keep.tile([P, PACK, HALF], BF16, name="z2a", tag="z2")
        nc.vector.tensor_tensor(flat(z2a[:, :last, :]), flat(picked[:]).bitcast(FP8), flat(scaled[0][:, :last, :]), MULT)
        nc.vector.tensor_tensor(z2a[:, last, :], tail[:].bitcast(FP8), scaled[0][:, last, :], MULT)
        later[2] = keep.tile([P, HALF], U8, name="later2", tag="picked")
        gather(1, 2, later[2][:])

        woven0 = [weave(0, 0, z1[0], nc.scalar.copy, "first0"), weave(0, 1, z2a, nc.vector.tensor_copy, "first1")]
        acc0 = multiply(0, woven0)
        scale(1, 3, later[3][:], on_scalar, on_scalar)
        woven11 = weave(1, 1, z2a, nc.scalar.copy, "woven11")
        woven10 = weave(1, 0, z1[0], nc.scalar.copy, "woven10")
        scale(1, 2, later[2][:], on_scalar, on_scalar)
        for t in (1, 0):
            later[t] = keep.tile([P, HALF], U8, name="later%d" % t, tag="first%d" % (1 - t), align_bytes=64)
            gather(1, t, later[t][:])
        sums0 = empty(0, acc0, nc.scalar.copy, "early")
        acc1 = multiply(1, [woven10, woven11])
        scale(1, 1, later[1][:], on_vector, on_vector)
        place(0, sums0)
        scale(1, 0, later[0][:], on_vector, on_vector)
        z2b = keep.tile([P, PACK, HALF], BF16, name="z2b", tag="z2")
        place(1, empty(1, acc1, nc.scalar.copy, "early"))
        for c in range(2, 4):
            cols = slice((c - 2) * CHUNK, (c - 1) * CHUNK)
            for t in (3, 2, 1, 0):
                nc.vector.tensor_tensor(z2b[:, t, cols], later[t][:, cols].bitcast(FP8), scaled[1][:, t, cols], MULT)
            woven = [weave(c, x, src, nc.vector.tensor_copy, "woven%d%d" % (c, x)) for x, src in enumerate((z1[1], z2b))]
            place(c, empty(c, multiply(c, woven), nc.vector.tensor_copy, "late%d" % c))
        nc.sync.dma_start(out[:P, :], pages[0][:])
        nc.sync.dma_start(out[P:, :], pages[1][:])
